import numpy as np
import ml_dtypes


def mxq(x, axis, fmt="e4m3"):
    dtype, down = {"e4m3": (ml_dtypes.float8_e4m3fn, 7), "e5m2": (ml_dtypes.float8_e5m2, 14)}[fmt]
    v = np.moveaxis(np.asarray(x, np.float32).astype(ml_dtypes.bfloat16).astype(np.float64), axis, -1)
    blocks = v.reshape(v.shape[:-1] + (-1, 32))
    amax = np.abs(blocks).max(-1, keepdims=True)
    byte = np.maximum(np.where(amax > 0, np.frexp(amax)[1] - 1 + 127, 0) - down, 1)
    scale = np.exp2(byte - 127.0)
    codes = (blocks / scale).astype(np.float32).astype(dtype).astype(np.float64)
    return np.moveaxis((codes * scale).reshape(v.shape), -1, axis)


WIDE = False


def mx_kscale(k):
    if not WIDE:
        return np.ones(k)
    levels = np.array([10, -10, 5, -5, 0])
    if k % 512:
        return np.exp2(np.random.permutation(np.resize(levels, k // 32))).repeat(32)
    a = np.empty((k // 512, 16))
    for p in range(k // 512):
        a[p, :8] = np.random.permutation(np.resize(levels, 8))
        for g in range(8):
            far = levels[np.abs(levels - a[p, g]) >= 10]
            a[p, g + 8] = far[np.random.randint(len(far))]
    return np.exp2(a.ravel()).repeat(32)


def f64(x):
    return np.asarray(x).astype(np.float64)


def striped8(idx):
    return np.asarray(idx).reshape(8, -1, 16).transpose(0, 2, 1).reshape(128, -1).astype(np.uint16)


def unstriped8(offs):
    return offs.reshape(8, 16, -1).transpose(0, 2, 1).reshape(8, -1).astype(np.int64)


def pick8(x, idx, run):
    r = np.arange(len(x))
    return x[r[:, None], idx[r % (8 * run) // run]]


E2M1 = np.array([0.0, 0.5, 1.0, 1.5, 2.0, 3.0, 4.0, 6.0, -0.0, -0.5, -1.0, -1.5, -2.0, -3.0, -4.0, -6.0])


def pack_weight(w, fmt):
    k, n = w.shape
    w = f64(np.asarray(w, np.float32).astype(ml_dtypes.bfloat16)).reshape(k // 32, 32, n)
    amax = np.abs(w).max(1)
    if fmt == "e4m3":
        byte = np.frexp(amax)[1] - 1 + 127 - 7
    else:
        mant, ex = np.frexp(amax / 6.0)
        byte = np.where(mant > 0.5, ex, ex - 1) + 127
    byte = np.clip(np.where(amax > 0, byte, 1), 1, 254)
    scaled = (w * np.exp2(127.0 - byte)[:, None, :]).reshape(k, n).astype(np.float32)
    by_word = np.ascontiguousarray(scaled.reshape(k // 512, 128, 4, n).transpose(0, 1, 3, 2))
    if fmt == "e4m3":
        words = by_word.astype(ml_dtypes.float8_e4m3fn).view(np.uint8)
    else:
        c = by_word.astype(ml_dtypes.float4_e2m1fn).view(np.uint8) & 0xF
        words = (c[..., 0::2] | (c[..., 1::2] << 4)).reshape(k // 512, 128, 2 * n)
    return np.ascontiguousarray(words), np.ascontiguousarray(byte.astype(np.uint8).reshape(k // 512, 16, n))


def unpack_weight(words, scales, fmt):
    g, _, n = scales.shape
    words = np.ascontiguousarray(words).reshape(g, 128, n, -1)
    if fmt == "e4m3":
        vals = words.view(ml_dtypes.float8_e4m3fn).astype(np.float64)
    else:
        nib = np.empty((g, 128, n, 4), np.uint8)
        nib[..., 0::2] = words & 0xF
        nib[..., 1::2] = words >> 4
        vals = E2M1[nib]
    vals = vals * np.repeat(np.exp2(scales.astype(np.float64) - 127.0), 8, axis=1)[..., None]
    return vals.transpose(0, 1, 3, 2).reshape(g * 512, n)


D, T, U, X, I, Q = 512, 1024, 1024, 1024, 512, 128


def setup_inputs():
    n = np.random.standard_normal
    idx = np.stack([np.random.permutation(T)[:I] for _ in range(8)])
    idx2 = np.stack([np.random.permutation(U)[:I] for _ in range(8)])
    idx3 = np.stack([np.random.permutation(U)[:I] for _ in range(8)])
    idx4 = np.stack([np.random.permutation(U)[:I] for _ in range(8)])
    idx5 = np.stack([np.random.permutation(X)[:I] for _ in range(8)])
    idx6 = np.stack([np.random.permutation(X)[:I] for _ in range(8)])
    fd = mx_kscale(D)
    keysp = pack_weight(n((D, T)) / fd[:, None], "e4m3")
    notesp = pack_weight(n((D, U)) / fd[:, None], "e2m1")
    usersp = pack_weight(n((D, X)) / fd[:, None], "e4m3")
    return {
        "query": (n((D, Q)) * 1.0 / np.sqrt(D) * fd[:, None]).astype(np.float32),
        "keys_words": keysp[0],
        "keys_scales": keysp[1],
        "notes_words": notesp[0],
        "notes_scales": notesp[1],
        "users_words": usersp[0],
        "users_scales": usersp[1],
        "offs": striped8(idx),
        "offs2": striped8(idx2),
        "offs3": striped8(idx3),
        "offs4": striped8(idx4),
        "offs5": striped8(idx5),
        "offs6": striped8(idx6),
    }


def reference(query, keys_words, keys_scales, notes_words, notes_scales, users_words, users_scales, offs, offs2, offs3, offs4, offs5, offs6):
    idx = unstriped8(offs)
    idx2 = unstriped8(offs2)
    idx3 = unstriped8(offs3)
    idx4 = unstriped8(offs4)
    idx5 = unstriped8(offs5)
    idx6 = unstriped8(offs6)
    keysu = unpack_weight(keys_words, keys_scales, "e4m3")
    notesu = unpack_weight(notes_words, notes_scales, "e2m1")
    usersu = unpack_weight(users_words, users_scales, "e4m3")
    queryq = mxq(f64(query), 0, "e4m3")
    a = queryq.T @ keysu
    b = queryq.T @ notesu
    c0 = queryq.T @ usersu
    m1 = np.maximum(pick8(a, idx, 16), pick8(b, idx2, 16))
    f1 = np.zeros((Q, U))
    f1[np.arange(Q)[:, None], idx3[np.arange(Q) % 128 // 16]] = m1
    bb = b + f1
    m2 = np.maximum(pick8(bb, idx4, 16), pick8(c0, idx5, 16))
    f2 = np.zeros((Q, X))
    f2[np.arange(Q)[:, None], idx6[np.arange(Q) % 128 // 16]] = m2
    cc = c0 + f2
    y = pick8(cc, idx5, 16)
    return y

@@ -1,0 +1,149 @@
+from contextlib import ExitStack
+
+import concourse.mybir as mybir
+
+F32 = mybir.dt.float32
+BF16 = mybir.dt.bfloat16
+I32 = mybir.dt.int32
+U32 = mybir.dt.uint32
+U16 = mybir.dt.uint16
+U8 = mybir.dt.uint8
+FP8X4 = mybir.dt.float8_e4m3fn_x4
+FP4X4 = mybir.dt.float4_e2m1fn_x4
+COPY = mybir.ActivationFunctionType.Copy
+MAX = mybir.AluOpType.max
+ADD = mybir.AluOpType.add
+
+P = 128
+PACK = 4
+POOL = 1024
+SLOTS = 512
+BANK = 512
+HALF = SLOTS // 2
+LIST_COLS = SLOTS // 16
+
+FLOPS = 2 * 512 * P * 3 * POOL
+
+
+def tile_attend_cascade_three_kernel(tc, query, keys_words, keys_scales, notes_words, notes_scales,
+                                      users_words, users_scales, offs, offs2, offs3, offs4, offs5, offs6, out):
+    nc = tc.nc
+    with ExitStack() as ctx:
+        held = ctx.enter_context(tc.tile_pool(name="held", bufs=1))
+        psum = ctx.enter_context(tc.psum_pool(name="psum", bufs=1))
+
+        def zeroed_plane(name):
+            plane = held.tile([P, POOL], U8, name=name, align_bytes=64)
+            nc.vector.memset(plane[:].bitcast(I32), 0)
+            return plane
+
+        def load_scales(queue, plane, scales):
+            rows = scales[0].bitcast(I32)
+            for quad in range(4):
+                queue.dma_start(out=plane[32 * quad : 32 * quad + 4, :].bitcast(I32),
+                                in_=rows[4 * quad : 4 * quad + 4, :])
+
+        def load_list(name, src):
+            tile = held.tile([P, LIST_COLS], U16, name=name)
+            nc.sync.dma_start(tile[:], src)
+            return tile
+
+        def half_of(lst, h):
+            return lst[:, h * LIST_COLS // 2 : (h + 1) * LIST_COLS // 2]
+
+        def slots(h):
+            return slice(h * HALF, (h + 1) * HALF)
+
+        notes_plane = zeroed_plane("notes_plane")
+        keys_plane = zeroed_plane("keys_plane")
+        users_plane = zeroed_plane("users_plane")
+
+        q_raw = held.tile([P, PACK, P], F32, name="q_raw")
+        nc.sync.dma_start(out=q_raw[:], in_=query.rearrange("(p j) q -> p j q", j=PACK))
+        notes_w = held.tile([P, 2 * POOL], U8, name="notes_w", align_bytes=64)
+        nc.sync.dma_start(out=notes_w[:].bitcast(I32), in_=notes_words[0].bitcast(I32))
+        load_scales(nc.scalar, notes_plane, notes_scales)
+        keys_w = held.tile([P, POOL], U32, name="keys_w", align_bytes=64)
+        nc.sync.dma_start(out=keys_w[:].bitcast(I32),
+                          in_=keys_words[0].rearrange("p n t -> p (n t)").bitcast(I32))
+        load_scales(nc.sync, keys_plane, keys_scales)
+        l2 = load_list("l2", offs2)
+        l1 = load_list("l1", offs)
+        l3 = load_list("l3", offs3)
+        users_w = held.tile([P, POOL], U32, name="users_w", align_bytes=64)
+        nc.sync.dma_start(out=users_w[:].bitcast(I32),
+                          in_=users_words[0].rearrange("p n t -> p (n t)").bitcast(I32))
+        load_scales(nc.sync, users_plane, users_scales)
+        l5 = load_list("l5", offs5)
+        l4 = load_list("l4", offs4)
+        l6 = load_list("l6", offs6)
+
+        f1 = held.tile([P, POOL], F32, name="f1")
+        f2 = held.tile([P, POOL], F32, name="f2")
+        nc.vector.memset(f1[:], 0.0)
+        nc.vector.memset(f2[:], 0.0)
+
+        q_bf = held.tile([P, P, PACK], BF16, name="q_bf", align_bytes=64)
+        nc.vector.tensor_copy(out=q_bf[:], in_=q_raw[:].rearrange("p j q -> p q j"))
+        q_codes = held.tile([P, P], U32, name="q_codes", align_bytes=64)
+        q_plane = held.tile([P, P], U8, name="q_plane", align_bytes=64)
+        nc.vector.quantize_mx(out=q_codes[:].bitcast(FP8X4), scales=q_plane[:],
+                              in_=q_bf[:].rearrange("p q j -> p (q j)"))
+
+        def score(name, rhs, rhs_scale, n):
+            bank = psum.tile([P, n], F32, name=name)
+            nc.tensor.matmul_mx(out=bank[:], lhsT=q_codes[:].bitcast(FP8X4), lhsT_scale=q_plane[:],
+                                rhs=rhs, rhs_scale=rhs_scale, start=True, stop=True)
+            return bank
+
+        b_ps = [score("b%d" % h, notes_w[:, 2 * BANK * h : 2 * BANK * (h + 1)].bitcast(FP4X4),
+                      notes_plane[:, BANK * h : BANK * (h + 1)], BANK) for h in range(2)]
+        a_cuts = [(0, 512), (512, 768), (768, 1024)]
+        a_ps = [score("a%d" % lo, keys_w[:, lo:hi].bitcast(FP8X4), keys_plane[:, lo:hi], hi - lo)
+                for lo, hi in a_cuts]
+        c_ps = [score("c%d" % h, users_w[:, BANK * h : BANK * (h + 1)].bitcast(FP8X4),
+                      users_plane[:, BANK * h : BANK * (h + 1)], BANK) for h in range(2)]
+
+        a = held.tile([P, POOL], F32, name="a")
+        b = held.tile([P, POOL], F32, name="b")
+        c0 = held.tile([P, POOL], F32, name="c0")
+        ga = held.tile([P, SLOTS], F32, name="ga")
+        gb = held.tile([P, SLOTS], F32, name="gb")
+        m1 = held.tile([P, SLOTS], F32, name="m1")
+
+        nc.scalar.copy(out=b[:, 0:BANK], in_=b_ps[0][:])
+        nc.vector.tensor_copy(out=b[:, BANK:POOL], in_=b_ps[1][:])
+        nc.scalar.activation(gb[:, slots(0)], b[:].indirect(half_of(l2, 0)), COPY)
+        nc.vector.tensor_copy(out=a[:, 0:512], in_=a_ps[0][:])
+        nc.scalar.copy(out=a[:, 512:768], in_=a_ps[1][:])
+        nc.vector.tensor_copy(out=a[:, 768:1024], in_=a_ps[2][:])
+        nc.vector.tensor_copy(ga[:, slots(0)], a[:].indirect(half_of(l1, 0)))
+        nc.scalar.activation(gb[:, slots(1)], b[:].indirect(half_of(l2, 1)), COPY)
+        nc.scalar.activation(ga[:, slots(1)], a[:].indirect(half_of(l1, 1)), COPY)
+        for h in range(2):
+            nc.vector.tensor_tensor(m1[:, slots(h)], ga[:, slots(h)], gb[:, slots(h)], MAX)
+            nc.vector.tensor_copy(f1[:].indirect(half_of(l3, h)), m1[:, slots(h)])
+
+        gc = held.tile([P, SLOTS], F32, name="gc")
+        for h in range(2):
+            nc.scalar.copy(out=c0[:, BANK * h : BANK * (h + 1)], in_=c_ps[h][:])
+        nc.scalar.activation(gc[:], c0[:].indirect(l5[:]), COPY)
+
+        bb = held.tile([P, POOL], F32, name="bb")
+        nc.vector.tensor_tensor(bb[:], b[:], f1[:], ADD)
+        gbb = held.tile([P, SLOTS], F32, name="gbb")
+        m2 = held.tile([P, SLOTS], F32, name="m2")
+        nc.vector.tensor_copy(gbb[:, slots(0)], bb[:].indirect(half_of(l4, 0)))
+        nc.scalar.activation(gbb[:, slots(1)], bb[:].indirect(half_of(l4, 1)), COPY)
+        for h in range(2):
+            nc.vector.tensor_tensor(m2[:, slots(h)], gbb[:, slots(h)], gc[:, slots(h)], MAX)
+        nc.vector.tensor_copy(f2[:].indirect(l6[:]), m2[:])
+
+        cc = held.tile([P, POOL], F32, name="cc")
+        nc.vector.tensor_tensor(cc[:], c0[:], f2[:], ADD)
+        y0 = held.tile([P, HALF], F32, name="y0")
+        y1 = held.tile([P, HALF], F32, name="y1")
+        nc.vector.tensor_copy(y0[:], cc[:].indirect(half_of(l5, 0)))
+        nc.scalar.activation(y1[:], cc[:].indirect(half_of(l5, 1)), COPY)
+        nc.sync.dma_start(out=out[:, slots(0)], in_=y0[:])
+        nc.scalar.dma_start(out=out[:, slots(1)], in_=y1[:])

@@ -34,7 +34,6 @@ def tile_attend_cascade_three_kernel(tc, query, keys_words, keys_scales, notes_w
 
         def zeroed_plane(name):
             plane = held.tile([P, POOL], U8, name=name, align_bytes=64)
-            nc.vector.memset(plane[:].bitcast(I32), 0)
             return plane
 
         def load_scales(queue, plane, scales):
@@ -84,11 +83,14 @@ def tile_attend_cascade_three_kernel(tc, query, keys_words, keys_scales, notes_w
         nc.vector.memset(f2[:], 0.0)
 
         q_bf = held.tile([P, P, PACK], BF16, name="q_bf", align_bytes=64)
-        nc.vector.tensor_copy(out=q_bf[:], in_=q_raw[:].rearrange("p j q -> p q j"))
         q_codes = held.tile([P, P], U32, name="q_codes", align_bytes=64)
         q_plane = held.tile([P, P], U8, name="q_plane", align_bytes=64)
-        nc.vector.quantize_mx(out=q_codes[:].bitcast(FP8X4), scales=q_plane[:],
-                              in_=q_bf[:].rearrange("p q j -> p (q j)"))
+        q_halves = [slice(0, P // 2), slice(P // 2, P)]
+        for cols in q_halves:
+            nc.vector.tensor_copy(out=q_bf[:, cols, :], in_=q_raw[:, :, cols].rearrange("p j q -> p q j"))
+        for cols in q_halves:
+            nc.vector.quantize_mx(out=q_codes[:, cols].bitcast(FP8X4), scales=q_plane[:, cols],
+                                  in_=q_bf[:, cols, :].rearrange("p q j -> p (q j)"))
 
         def score(name, rhs, rhs_scale, n):
             bank = psum.tile([P, n], F32, name=name)
@@ -106,41 +108,43 @@ def tile_attend_cascade_three_kernel(tc, query, keys_words, keys_scales, notes_w
 
         a = held.tile([P, POOL], F32, name="a")
         b = held.tile([P, POOL], F32, name="b")
-        c0 = held.tile([P, POOL], F32, name="c0")
-        ga = held.tile([P, SLOTS], F32, name="ga")
-        gb = held.tile([P, SLOTS], F32, name="gb")
-        m1 = held.tile([P, SLOTS], F32, name="m1")
+        c0 = held.tile([P, POOL], F32, name="table")
+        ga = [held.tile([P, HALF], F32, name="ga%d" % h) for h in range(2)]
+        gb = [held.tile([P, HALF], F32, name="gb%d" % h) for h in range(2)]
 
         nc.scalar.copy(out=b[:, 0:BANK], in_=b_ps[0][:])
         nc.vector.tensor_copy(out=b[:, BANK:POOL], in_=b_ps[1][:])
-        nc.scalar.activation(gb[:, slots(0)], b[:].indirect(half_of(l2, 0)), COPY)
-        nc.vector.tensor_copy(out=a[:, 0:512], in_=a_ps[0][:])
-        nc.scalar.copy(out=a[:, 512:768], in_=a_ps[1][:])
+        nc.scalar.copy(out=a[:, 0:512], in_=a_ps[0][:])
+        nc.vector.tensor_copy(out=a[:, 512:768], in_=a_ps[1][:])
         nc.vector.tensor_copy(out=a[:, 768:1024], in_=a_ps[2][:])
-        nc.vector.tensor_copy(ga[:, slots(0)], a[:].indirect(half_of(l1, 0)))
-        nc.scalar.activation(gb[:, slots(1)], b[:].indirect(half_of(l2, 1)), COPY)
-        nc.scalar.activation(ga[:, slots(1)], a[:].indirect(half_of(l1, 1)), COPY)
+        nc.scalar.activation(gb[0][:], b[:].indirect(half_of(l2, 0)), COPY)
+        nc.vector.tensor_copy(ga[0][:], a[:].indirect(half_of(l1, 0)))
+        nc.scalar.activation(gb[1][:], b[:].indirect(half_of(l2, 1)), COPY)
+        nc.scalar.activation(ga[1][:], a[:].indirect(half_of(l1, 1)), COPY)
         for h in range(2):
-            nc.vector.tensor_tensor(m1[:, slots(h)], ga[:, slots(h)], gb[:, slots(h)], MAX)
-            nc.vector.tensor_copy(f1[:].indirect(half_of(l3, h)), m1[:, slots(h)])
+            m1 = held.tile([P, HALF], F32, name="m1")
+            nc.vector.tensor_tensor(m1[:], ga[h][:], gb[h][:], MAX)
+            nc.vector.tensor_copy(f1[:].indirect(half_of(l3, h)), m1[:])
 
         gc = held.tile([P, SLOTS], F32, name="gc")
         for h in range(2):
             nc.scalar.copy(out=c0[:, BANK * h : BANK * (h + 1)], in_=c_ps[h][:])
         nc.scalar.activation(gc[:], c0[:].indirect(l5[:]), COPY)
 
-        bb = held.tile([P, POOL], F32, name="bb")
+        bb = held.tile([P, POOL], F32, name="table")
         nc.vector.tensor_tensor(bb[:], b[:], f1[:], ADD)
-        gbb = held.tile([P, SLOTS], F32, name="gbb")
+        gbb = [held.tile([P, HALF], F32, name="gbb%d" % h) for h in range(2)]
         m2 = held.tile([P, SLOTS], F32, name="m2")
-        nc.vector.tensor_copy(gbb[:, slots(0)], bb[:].indirect(half_of(l4, 0)))
-        nc.scalar.activation(gbb[:, slots(1)], bb[:].indirect(half_of(l4, 1)), COPY)
+        nc.vector.tensor_copy(gbb[0][:], bb[:].indirect(half_of(l4, 0)))
+        nc.scalar.activation(gbb[1][:], bb[:].indirect(half_of(l4, 1)), COPY)
         for h in range(2):
-            nc.vector.tensor_tensor(m2[:, slots(h)], gbb[:, slots(h)], gc[:, slots(h)], MAX)
+            nc.vector.tensor_tensor(m2[:, slots(h)], gbb[h][:], gc[:, slots(h)], MAX)
         nc.vector.tensor_copy(f2[:].indirect(l6[:]), m2[:])
 
         cc = held.tile([P, POOL], F32, name="cc")
-        nc.vector.tensor_tensor(cc[:], c0[:], f2[:], ADD)
+        for h in range(2):
+            cols = slice(BANK * h, BANK * (h + 1))
+            nc.vector.tensor_tensor(cc[:, cols], c_ps[h][:], f2[:, cols], ADD)
         y0 = held.tile([P, HALF], F32, name="y0")
         y1 = held.tile([P, HALF], F32, name="y1")
         nc.vector.tensor_copy(y0[:], cc[:].indirect(half_of(l5, 0)))

@@ -32,15 +32,19 @@ def tile_attend_cascade_three_kernel(tc, query, keys_words, keys_scales, notes_w
         held = ctx.enter_context(tc.tile_pool(name="held", bufs=1))
         psum = ctx.enter_context(tc.psum_pool(name="psum", bufs=1))
 
-        def zeroed_plane(name):
+        def load_scales(name, scales, first):
             plane = held.tile([P, POOL], U8, name=name, align_bytes=64)
-            return plane
-
-        def load_scales(queue, plane, scales):
             rows = scales[0].bitcast(I32)
             for quad in range(4):
-                queue.dma_start(out=plane[32 * quad : 32 * quad + 4, :].bitcast(I32),
-                                in_=rows[4 * quad : 4 * quad + 4, :])
+                top = 32 * quad + first
+                nc.sync.dma_start(out=plane[top : top + 4, :].bitcast(I32), in_=rows[4 * quad : 4 * quad + 4, :])
+            return plane[first:P, :]
+
+        def load_words(name, words):
+            tile = held.tile([P, POOL], U32, name=name, align_bytes=64)
+            nc.sync.dma_start(out=tile[:].bitcast(I32),
+                              in_=words[0].rearrange("p n t -> p (n t)").bitcast(I32))
+            return tile
 
         def load_list(name, src):
             tile = held.tile([P, LIST_COLS], U16, name=name)
@@ -53,26 +57,18 @@ def tile_attend_cascade_three_kernel(tc, query, keys_words, keys_scales, notes_w
         def slots(h):
             return slice(h * HALF, (h + 1) * HALF)
 
-        notes_plane = zeroed_plane("notes_plane")
-        keys_plane = zeroed_plane("keys_plane")
-        users_plane = zeroed_plane("users_plane")
-
         q_raw = held.tile([P, PACK, P], F32, name="q_raw")
         nc.sync.dma_start(out=q_raw[:], in_=query.rearrange("(p j) q -> p j q", j=PACK))
+        notes_plane = load_scales("notes_plane", notes_scales, 0)
         notes_w = held.tile([P, 2 * POOL], U8, name="notes_w", align_bytes=64)
         nc.sync.dma_start(out=notes_w[:].bitcast(I32), in_=notes_words[0].bitcast(I32))
-        load_scales(nc.scalar, notes_plane, notes_scales)
-        keys_w = held.tile([P, POOL], U32, name="keys_w", align_bytes=64)
-        nc.sync.dma_start(out=keys_w[:].bitcast(I32),
-                          in_=keys_words[0].rearrange("p n t -> p (n t)").bitcast(I32))
-        load_scales(nc.sync, keys_plane, keys_scales)
+        keys_w = load_words("keys_w", keys_words)
+        keys_plane = load_scales("keys_plane", keys_scales, 4)
         l2 = load_list("l2", offs2)
         l1 = load_list("l1", offs)
         l3 = load_list("l3", offs3)
-        users_w = held.tile([P, POOL], U32, name="users_w", align_bytes=64)
-        nc.sync.dma_start(out=users_w[:].bitcast(I32),
-                          in_=users_words[0].rearrange("p n t -> p (n t)").bitcast(I32))
-        load_scales(nc.sync, users_plane, users_scales)
+        users_w = load_words("users_w", users_words)
+        users_plane = load_scales("users_plane", users_scales, 8)
         l5 = load_list("l5", offs5)
         l4 = load_list("l4", offs4)
         l6 = load_list("l6", offs6)
@@ -110,21 +106,19 @@ def tile_attend_cascade_three_kernel(tc, query, keys_words, keys_scales, notes_w
         b = held.tile([P, POOL], F32, name="b")
         c0 = held.tile([P, POOL], F32, name="table")
         ga = [held.tile([P, HALF], F32, name="ga%d" % h) for h in range(2)]
-        gb = [held.tile([P, HALF], F32, name="gb%d" % h) for h in range(2)]
+        gb = held.tile([P, SLOTS], F32, name="gb")
+        m1 = held.tile([P, SLOTS], F32, name="m1")
 
         nc.scalar.copy(out=b[:, 0:BANK], in_=b_ps[0][:])
         nc.vector.tensor_copy(out=b[:, BANK:POOL], in_=b_ps[1][:])
-        nc.scalar.copy(out=a[:, 0:512], in_=a_ps[0][:])
-        nc.vector.tensor_copy(out=a[:, 512:768], in_=a_ps[1][:])
-        nc.vector.tensor_copy(out=a[:, 768:1024], in_=a_ps[2][:])
-        nc.scalar.activation(gb[0][:], b[:].indirect(half_of(l2, 0)), COPY)
-        nc.vector.tensor_copy(ga[0][:], a[:].indirect(half_of(l1, 0)))
-        nc.scalar.activation(gb[1][:], b[:].indirect(half_of(l2, 1)), COPY)
-        nc.scalar.activation(ga[1][:], a[:].indirect(half_of(l1, 1)), COPY)
+        nc.scalar.activation(gb[:], b[:].indirect(l2[:]), COPY)
+        for (lo, hi), bank in zip(a_cuts, a_ps):
+            nc.vector.tensor_copy(out=a[:, lo:hi], in_=bank[:])
+        nc.scalar.activation(ga[0][:], a[:].indirect(half_of(l1, 0)), COPY)
+        nc.vector.tensor_copy(ga[1][:], a[:].indirect(half_of(l1, 1)))
         for h in range(2):
-            m1 = held.tile([P, HALF], F32, name="m1")
-            nc.vector.tensor_tensor(m1[:], ga[h][:], gb[h][:], MAX)
-            nc.vector.tensor_copy(f1[:].indirect(half_of(l3, h)), m1[:])
+            nc.vector.tensor_tensor(m1[:, slots(h)], ga[h][:], gb[:, slots(h)], MAX)
+        nc.vector.tensor_copy(f1[:].indirect(l3[:]), m1[:])
 
         gc = held.tile([P, SLOTS], F32, name="gc")
         for h in range(2):
@@ -135,8 +129,8 @@ def tile_attend_cascade_three_kernel(tc, query, keys_words, keys_scales, notes_w
         nc.vector.tensor_tensor(bb[:], b[:], f1[:], ADD)
         gbb = [held.tile([P, HALF], F32, name="gbb%d" % h) for h in range(2)]
         m2 = held.tile([P, SLOTS], F32, name="m2")
-        nc.vector.tensor_copy(gbb[0][:], bb[:].indirect(half_of(l4, 0)))
-        nc.scalar.activation(gbb[1][:], bb[:].indirect(half_of(l4, 1)), COPY)
+        nc.scalar.activation(gbb[0][:], bb[:].indirect(half_of(l4, 0)), COPY)
+        nc.vector.tensor_copy(gbb[1][:], bb[:].indirect(half_of(l4, 1)))
         for h in range(2):
             nc.vector.tensor_tensor(m2[:, slots(h)], gbb[h][:], gc[:, slots(h)], MAX)
         nc.vector.tensor_copy(f2[:].indirect(l6[:]), m2[:])

@@ -21,6 +21,7 @@ SLOTS = 512
 BANK = 512
 HALF = SLOTS // 2
 LIST_COLS = SLOTS // 16
+TAIL = 256
 
 FLOPS = 2 * 512 * P * 3 * POOL
 
@@ -94,26 +95,27 @@ def tile_attend_cascade_three_kernel(tc, query, keys_words, keys_scales, notes_w
                                 rhs=rhs, rhs_scale=rhs_scale, start=True, stop=True)
             return bank
 
-        b_ps = [score("b%d" % h, notes_w[:, 2 * BANK * h : 2 * BANK * (h + 1)].bitcast(FP4X4),
-                      notes_plane[:, BANK * h : BANK * (h + 1)], BANK) for h in range(2)]
-        a_cuts = [(0, 512), (512, 768), (768, 1024)]
-        a_ps = [score("a%d" % lo, keys_w[:, lo:hi].bitcast(FP8X4), keys_plane[:, lo:hi], hi - lo)
-                for lo, hi in a_cuts]
+        cuts = [slice(0, 512), slice(512, 768), slice(768, 1024)]
+        b_ps = [score("b%d" % c.start, notes_w[:, 2 * c.start : 2 * c.stop].bitcast(FP4X4),
+                      notes_plane[:, c], c.stop - c.start) for c in cuts]
+        a_ps = [score("a%d" % c.start, keys_w[:, c].bitcast(FP8X4), keys_plane[:, c], c.stop - c.start)
+                for c in cuts]
         c_ps = [score("c%d" % h, users_w[:, BANK * h : BANK * (h + 1)].bitcast(FP8X4),
                       users_plane[:, BANK * h : BANK * (h + 1)], BANK) for h in range(2)]
 
         a = held.tile([P, POOL], F32, name="a")
         b = held.tile([P, POOL], F32, name="b")
-        c0 = held.tile([P, POOL], F32, name="table")
+        c0 = held.tile([P, POOL], F32, name="c0")
         ga = [held.tile([P, HALF], F32, name="ga%d" % h) for h in range(2)]
         gb = held.tile([P, SLOTS], F32, name="gb")
         m1 = held.tile([P, SLOTS], F32, name="m1")
 
-        nc.scalar.copy(out=b[:, 0:BANK], in_=b_ps[0][:])
-        nc.vector.tensor_copy(out=b[:, BANK:POOL], in_=b_ps[1][:])
+        nc.scalar.copy(out=b[:, cuts[0]], in_=b_ps[0][:])
+        nc.vector.tensor_copy(out=b[:, cuts[1]], in_=b_ps[1][:])
+        nc.scalar.copy(out=b[:, cuts[2]], in_=b_ps[2][:])
         nc.scalar.activation(gb[:], b[:].indirect(l2[:]), COPY)
-        for (lo, hi), bank in zip(a_cuts, a_ps):
-            nc.vector.tensor_copy(out=a[:, lo:hi], in_=bank[:])
+        for c, bank in zip(cuts, a_ps):
+            nc.vector.tensor_copy(out=a[:, c], in_=bank[:])
         nc.scalar.activation(ga[0][:], a[:].indirect(half_of(l1, 0)), COPY)
         nc.vector.tensor_copy(ga[1][:], a[:].indirect(half_of(l1, 1)))
         for h in range(2):
@@ -121,13 +123,17 @@ def tile_attend_cascade_three_kernel(tc, query, keys_words, keys_scales, notes_w
         nc.vector.tensor_copy(f1[:].indirect(l3[:]), m1[:])
 
         gc = held.tile([P, SLOTS], F32, name="gc")
+        c_tail = held.tile([P, TAIL], F32, name="c_tail")
         for h in range(2):
             nc.scalar.copy(out=c0[:, BANK * h : BANK * (h + 1)], in_=c_ps[h][:])
         nc.scalar.activation(gc[:], c0[:].indirect(l5[:]), COPY)
+        nc.scalar.copy(out=c_tail[:], in_=c_ps[1][:, BANK - TAIL : BANK])
 
-        bb = held.tile([P, POOL], F32, name="table")
-        nc.vector.tensor_tensor(bb[:], b[:], f1[:], ADD)
-        gbb = [held.tile([P, HALF], F32, name="gbb%d" % h) for h in range(2)]
+        bb = held.tile([P, POOL], F32, name="bb")
+        nc.gpsimd.tensor_tensor(bb[:, cuts[2]], b[:, cuts[2]], f1[:, cuts[2]], ADD)
+        for h in range(2):
+            nc.vector.tensor_tensor(bb[:, cuts[h]], b_ps[h][:], f1[:, cuts[h]], ADD)
+        gbb = [held.tile([P, HALF], F32, name=name) for name in ("c0", "gbb1")]
         m2 = held.tile([P, SLOTS], F32, name="m2")
         nc.scalar.activation(gbb[0][:], bb[:].indirect(half_of(l4, 0)), COPY)
         nc.vector.tensor_copy(gbb[1][:], bb[:].indirect(half_of(l4, 1)))
@@ -136,9 +142,9 @@ def tile_attend_cascade_three_kernel(tc, query, keys_words, keys_scales, notes_w
         nc.vector.tensor_copy(f2[:].indirect(l6[:]), m2[:])
 
         cc = held.tile([P, POOL], F32, name="cc")
-        for h in range(2):
-            cols = slice(BANK * h, BANK * (h + 1))
-            nc.vector.tensor_tensor(cc[:, cols], c_ps[h][:], f2[:, cols], ADD)
+        nc.gpsimd.tensor_tensor(cc[:, cuts[2]], c_tail[:], f2[:, cuts[2]], ADD)
+        nc.vector.tensor_tensor(cc[:, cuts[0]], c_ps[0][:], f2[:, cuts[0]], ADD)
+        nc.vector.tensor_tensor(cc[:, cuts[1]], c_ps[1][:, 0 : BANK - TAIL], f2[:, cuts[1]], ADD)
         y0 = held.tile([P, HALF], F32, name="y0")
         y1 = held.tile([P, HALF], F32, name="y1")
         nc.vector.tensor_copy(y0[:], cc[:].indirect(half_of(l5, 0)))

@@ -16,14 +16,17 @@ ADD = mybir.AluOpType.add
 
 P = 128
 PACK = 4
+FEATURES = P * PACK
+QUADRANT = 32
+SCALE_ROWS = 4
 POOL = 1024
 SLOTS = 512
-BANK = 512
 HALF = SLOTS // 2
 LIST_COLS = SLOTS // 16
-TAIL = 256
+BANK = 512
+TAIL = POOL // 4
 
-FLOPS = 2 * 512 * P * 3 * POOL
+FLOPS = 2 * FEATURES * P * 3 * POOL
 
 
 def tile_attend_cascade_three_kernel(tc, query, keys_words, keys_scales, notes_words, notes_scales,
@@ -34,14 +37,15 @@ def tile_attend_cascade_three_kernel(tc, query, keys_words, keys_scales, notes_w
         psum = ctx.enter_context(tc.psum_pool(name="psum", bufs=1))
 
         def load_scales(name, scales, first):
-            plane = held.tile([P, POOL], U8, name=name, align_bytes=64)
+            tile = held.tile([P, POOL], U8, name=name, align_bytes=64)
             rows = scales[0].bitcast(I32)
-            for quad in range(4):
-                top = 32 * quad + first
-                nc.sync.dma_start(out=plane[top : top + 4, :].bitcast(I32), in_=rows[4 * quad : 4 * quad + 4, :])
-            return plane[first:P, :]
+            for quad in range(P // QUADRANT):
+                top = QUADRANT * quad + first
+                nc.sync.dma_start(out=tile[top : top + SCALE_ROWS, :].bitcast(I32),
+                                  in_=rows[SCALE_ROWS * quad : SCALE_ROWS * (quad + 1), :])
+            return tile[first:P, :]
 
-        def load_words(name, words):
+        def load_e4m3_words(name, words):
             tile = held.tile([P, POOL], U32, name=name, align_bytes=64)
             nc.sync.dma_start(out=tile[:].bitcast(I32),
                               in_=words[0].rearrange("p n t -> p (n t)").bitcast(I32))
@@ -52,27 +56,27 @@ def tile_attend_cascade_three_kernel(tc, query, keys_words, keys_scales, notes_w
             nc.sync.dma_start(tile[:], src)
             return tile
 
-        def half_of(lst, h):
-            return lst[:, h * LIST_COLS // 2 : (h + 1) * LIST_COLS // 2]
+        def list_half(tile, h):
+            return tile[:, h * LIST_COLS // 2 : (h + 1) * LIST_COLS // 2]
 
-        def slots(h):
+        def slot_half(h):
             return slice(h * HALF, (h + 1) * HALF)
 
         q_raw = held.tile([P, PACK, P], F32, name="q_raw")
-        nc.sync.dma_start(out=q_raw[:], in_=query.rearrange("(p j) q -> p j q", j=PACK))
-        notes_plane = load_scales("notes_plane", notes_scales, 0)
+        nc.sync.dma_start(out=q_raw[:], in_=query.rearrange("(p t) q -> p t q", t=PACK))
+        notes_sc = load_scales("notes_sc", notes_scales, 0)
         notes_w = held.tile([P, 2 * POOL], U8, name="notes_w", align_bytes=64)
         nc.sync.dma_start(out=notes_w[:].bitcast(I32), in_=notes_words[0].bitcast(I32))
-        keys_w = load_words("keys_w", keys_words)
-        keys_plane = load_scales("keys_plane", keys_scales, 4)
-        l2 = load_list("l2", offs2)
-        l1 = load_list("l1", offs)
-        l3 = load_list("l3", offs3)
-        users_w = load_words("users_w", users_words)
-        users_plane = load_scales("users_plane", users_scales, 8)
-        l5 = load_list("l5", offs5)
-        l4 = load_list("l4", offs4)
-        l6 = load_list("l6", offs6)
+        keys_w = load_e4m3_words("keys_w", keys_words)
+        keys_sc = load_scales("keys_sc", keys_scales, SCALE_ROWS)
+        idx2 = load_list("idx2", offs2)
+        idx = load_list("idx", offs)
+        idx3 = load_list("idx3", offs3)
+        users_w = load_e4m3_words("users_w", users_words)
+        users_sc = load_scales("users_sc", users_scales, 2 * SCALE_ROWS)
+        idx5 = load_list("idx5", offs5)
+        idx4 = load_list("idx4", offs4)
+        idx6 = load_list("idx6", offs6)
 
         f1 = held.tile([P, POOL], F32, name="f1")
         f2 = held.tile([P, POOL], F32, name="f2")
@@ -80,74 +84,77 @@ def tile_attend_cascade_three_kernel(tc, query, keys_words, keys_scales, notes_w
         nc.vector.memset(f2[:], 0.0)
 
         q_bf = held.tile([P, P, PACK], BF16, name="q_bf", align_bytes=64)
-        q_codes = held.tile([P, P], U32, name="q_codes", align_bytes=64)
-        q_plane = held.tile([P, P], U8, name="q_plane", align_bytes=64)
-        q_halves = [slice(0, P // 2), slice(P // 2, P)]
-        for cols in q_halves:
-            nc.vector.tensor_copy(out=q_bf[:, cols, :], in_=q_raw[:, :, cols].rearrange("p j q -> p q j"))
-        for cols in q_halves:
-            nc.vector.quantize_mx(out=q_codes[:, cols].bitcast(FP8X4), scales=q_plane[:, cols],
-                                  in_=q_bf[:, cols, :].rearrange("p q j -> p (q j)"))
+        q_w = held.tile([P, P], U32, name="q_w", align_bytes=64)
+        q_sc = held.tile([P, P], U8, name="q_sc", align_bytes=64)
+        row_halves = [slice(0, P // 2), slice(P // 2, P)]
+        for rows in row_halves:
+            nc.vector.tensor_copy(out=q_bf[:, rows, :], in_=q_raw[:, :, rows].rearrange("p t q -> p q t"))
+        for rows in row_halves:
+            nc.vector.quantize_mx(out=q_w[:, rows].bitcast(FP8X4), scales=q_sc[:, rows],
+                                  in_=q_bf[:, rows, :].rearrange("p q t -> p (q t)"))
 
-        def score(name, rhs, rhs_scale, n):
-            bank = psum.tile([P, n], F32, name=name)
-            nc.tensor.matmul_mx(out=bank[:], lhsT=q_codes[:].bitcast(FP8X4), lhsT_scale=q_plane[:],
-                                rhs=rhs, rhs_scale=rhs_scale, start=True, stop=True)
+        def score(bank_name, words, scales):
+            bank = psum.tile([P, scales.shape[1]], F32, name=bank_name)
+            nc.tensor.matmul_mx(out=bank[:], lhsT=q_w[:].bitcast(FP8X4), lhsT_scale=q_sc[:],
+                                rhs=words, rhs_scale=scales, start=True, stop=True)
             return bank
 
-        cuts = [slice(0, 512), slice(512, 768), slice(768, 1024)]
-        b_ps = [score("b%d" % c.start, notes_w[:, 2 * c.start : 2 * c.stop].bitcast(FP4X4),
-                      notes_plane[:, c], c.stop - c.start) for c in cuts]
-        a_ps = [score("a%d" % c.start, keys_w[:, c].bitcast(FP8X4), keys_plane[:, c], c.stop - c.start)
-                for c in cuts]
-        c_ps = [score("c%d" % h, users_w[:, BANK * h : BANK * (h + 1)].bitcast(FP8X4),
-                      users_plane[:, BANK * h : BANK * (h + 1)], BANK) for h in range(2)]
+        pieces = [slice(0, BANK), slice(BANK, POOL - TAIL), slice(POOL - TAIL, POOL)]
+        b_ps = [score("b%d" % n, notes_w[:, 2 * cols.start : 2 * cols.stop].bitcast(FP4X4), notes_sc[:, cols])
+                for n, cols in enumerate(pieces)]
+        quarters = [slice(lo, lo + POOL // 4) for lo in range(0, POOL, POOL // 4)]
+        a_ps = [score("ac%d" % n, keys_w[:, cols].bitcast(FP8X4), keys_sc[:, cols])
+                for n, cols in enumerate(quarters)]
 
         a = held.tile([P, POOL], F32, name="a")
         b = held.tile([P, POOL], F32, name="b")
         c0 = held.tile([P, POOL], F32, name="c0")
-        ga = [held.tile([P, HALF], F32, name="ga%d" % h) for h in range(2)]
-        gb = held.tile([P, SLOTS], F32, name="gb")
+        a_got = [held.tile([P, HALF], F32, name="a_got%d" % h) for h in range(2)]
+        b_got = held.tile([P, SLOTS], F32, name="b_got")
         m1 = held.tile([P, SLOTS], F32, name="m1")
 
-        nc.scalar.copy(out=b[:, cuts[0]], in_=b_ps[0][:])
-        nc.vector.tensor_copy(out=b[:, cuts[1]], in_=b_ps[1][:])
-        nc.scalar.copy(out=b[:, cuts[2]], in_=b_ps[2][:])
-        nc.scalar.activation(gb[:], b[:].indirect(l2[:]), COPY)
-        for c, bank in zip(cuts, a_ps):
-            nc.vector.tensor_copy(out=a[:, c], in_=bank[:])
-        nc.scalar.activation(ga[0][:], a[:].indirect(half_of(l1, 0)), COPY)
-        nc.vector.tensor_copy(ga[1][:], a[:].indirect(half_of(l1, 1)))
+        nc.scalar.copy(out=b[:, pieces[0]], in_=b_ps[0][:])
+        nc.vector.tensor_copy(out=b[:, pieces[1]], in_=b_ps[1][:])
+        nc.scalar.copy(out=b[:, pieces[2]], in_=b_ps[2][:])
+        nc.scalar.activation(b_got[:], b[:].indirect(idx2[:]), COPY)
+        for cols, bank in zip(quarters, a_ps):
+            nc.vector.tensor_copy(out=a[:, cols], in_=bank[:])
+        nc.scalar.activation(a_got[0][:], a[:].indirect(list_half(idx, 0)), COPY)
+        nc.vector.tensor_copy(a_got[1][:], a[:].indirect(list_half(idx, 1)))
         for h in range(2):
-            nc.vector.tensor_tensor(m1[:, slots(h)], ga[h][:], gb[:, slots(h)], MAX)
-        nc.vector.tensor_copy(f1[:].indirect(l3[:]), m1[:])
+            nc.vector.tensor_tensor(m1[:, slot_half(h)], a_got[h][:], b_got[:, slot_half(h)], MAX)
+        nc.vector.tensor_copy(f1[:].indirect(idx3[:]), m1[:])
 
-        gc = held.tile([P, SLOTS], F32, name="gc")
-        c_tail = held.tile([P, TAIL], F32, name="c_tail")
-        for h in range(2):
-            nc.scalar.copy(out=c0[:, BANK * h : BANK * (h + 1)], in_=c_ps[h][:])
-        nc.scalar.activation(gc[:], c0[:].indirect(l5[:]), COPY)
-        nc.scalar.copy(out=c_tail[:], in_=c_ps[1][:, BANK - TAIL : BANK])
+        banks = [slice(0, BANK), slice(BANK, POOL)]
+        c_ps = [score("ac%d" % n, users_w[:, cols].bitcast(FP8X4), users_sc[:, cols])
+                for n, cols in enumerate(banks)]
+
+        c0_got = held.tile([P, SLOTS], F32, name="c0_got")
+        c0_tail = held.tile([P, TAIL], F32, name="c0_tail")
+        for cols, bank in zip(banks, c_ps):
+            nc.scalar.copy(out=c0[:, cols], in_=bank[:])
+        nc.scalar.activation(c0_got[:], c0[:].indirect(idx5[:]), COPY)
+        nc.scalar.copy(out=c0_tail[:], in_=c_ps[1][:, BANK - TAIL : BANK])
 
         bb = held.tile([P, POOL], F32, name="bb")
-        nc.gpsimd.tensor_tensor(bb[:, cuts[2]], b[:, cuts[2]], f1[:, cuts[2]], ADD)
-        for h in range(2):
-            nc.vector.tensor_tensor(bb[:, cuts[h]], b_ps[h][:], f1[:, cuts[h]], ADD)
-        gbb = [held.tile([P, HALF], F32, name=name) for name in ("c0", "gbb1")]
+        nc.gpsimd.tensor_tensor(bb[:, pieces[2]], b[:, pieces[2]], f1[:, pieces[2]], ADD)
+        for n in range(2):
+            nc.vector.tensor_tensor(bb[:, pieces[n]], b_ps[n][:], f1[:, pieces[n]], ADD)
+
+        bb_got = [held.tile([P, HALF], F32, name=name) for name in ("c0", "bb_got1")]
         m2 = held.tile([P, SLOTS], F32, name="m2")
-        nc.scalar.activation(gbb[0][:], bb[:].indirect(half_of(l4, 0)), COPY)
-        nc.vector.tensor_copy(gbb[1][:], bb[:].indirect(half_of(l4, 1)))
+        nc.scalar.activation(bb_got[0][:], bb[:].indirect(list_half(idx4, 0)), COPY)
+        nc.vector.tensor_copy(bb_got[1][:], bb[:].indirect(list_half(idx4, 1)))
         for h in range(2):
-            nc.vector.tensor_tensor(m2[:, slots(h)], gbb[h][:], gc[:, slots(h)], MAX)
-        nc.vector.tensor_copy(f2[:].indirect(l6[:]), m2[:])
+            nc.vector.tensor_tensor(m2[:, slot_half(h)], bb_got[h][:], c0_got[:, slot_half(h)], MAX)
+        nc.vector.tensor_copy(f2[:].indirect(idx6[:]), m2[:])
 
         cc = held.tile([P, POOL], F32, name="cc")
-        nc.gpsimd.tensor_tensor(cc[:, cuts[2]], c_tail[:], f2[:, cuts[2]], ADD)
-        nc.vector.tensor_tensor(cc[:, cuts[0]], c_ps[0][:], f2[:, cuts[0]], ADD)
-        nc.vector.tensor_tensor(cc[:, cuts[1]], c_ps[1][:, 0 : BANK - TAIL], f2[:, cuts[1]], ADD)
-        y0 = held.tile([P, HALF], F32, name="y0")
-        y1 = held.tile([P, HALF], F32, name="y1")
-        nc.vector.tensor_copy(y0[:], cc[:].indirect(half_of(l5, 0)))
-        nc.scalar.activation(y1[:], cc[:].indirect(half_of(l5, 1)), COPY)
-        nc.sync.dma_start(out=out[:, slots(0)], in_=y0[:])
-        nc.scalar.dma_start(out=out[:, slots(1)], in_=y1[:])
+        nc.gpsimd.tensor_tensor(cc[:, pieces[2]], c0_tail[:], f2[:, pieces[2]], ADD)
+        nc.vector.tensor_tensor(cc[:, pieces[0]], c_ps[0][:], f2[:, pieces[0]], ADD)
+        nc.vector.tensor_tensor(cc[:, pieces[1]], c_ps[1][:, 0 : BANK - TAIL], f2[:, pieces[1]], ADD)
+        result = [held.tile([P, HALF], F32, name="result%d" % h) for h in range(2)]
+        nc.vector.tensor_copy(result[0][:], cc[:].indirect(list_half(idx5, 0)))
+        nc.scalar.activation(result[1][:], cc[:].indirect(list_half(idx5, 1)), COPY)
+        nc.sync.dma_start(out=out[:, slot_half(0)], in_=result[0][:])
+        nc.scalar.dma_start(out=out[:, slot_half(1)], in_=result[1][:])

from contextlib import ExitStack

import concourse.mybir as mybir

F32 = mybir.dt.float32
BF16 = mybir.dt.bfloat16
I32 = mybir.dt.int32
U32 = mybir.dt.uint32
U16 = mybir.dt.uint16
U8 = mybir.dt.uint8
FP8X4 = mybir.dt.float8_e4m3fn_x4
FP4X4 = mybir.dt.float4_e2m1fn_x4
COPY = mybir.ActivationFunctionType.Copy
MAX = mybir.AluOpType.max
ADD = mybir.AluOpType.add

P = 128
PACK = 4
FEATURES = P * PACK
QUADRANT = 32
SCALE_ROWS = 4
POOL = 1024
SLOTS = 512
HALF = SLOTS // 2
LIST_COLS = SLOTS // 16
BANK = 512
TAIL = POOL // 4

FLOPS = 2 * FEATURES * P * 3 * POOL


def tile_attend_cascade_three_kernel(tc, query, keys_words, keys_scales, notes_words, notes_scales,
                                      users_words, users_scales, offs, offs2, offs3, offs4, offs5, offs6, out):
    nc = tc.nc
    with ExitStack() as ctx:
        held = ctx.enter_context(tc.tile_pool(name="held", bufs=1))
        psum = ctx.enter_context(tc.psum_pool(name="psum", bufs=1))

        def load_scales(name, scales, first):
            tile = held.tile([P, POOL], U8, name=name, align_bytes=64)
            rows = scales[0].bitcast(I32)
            for quad in range(P // QUADRANT):
                top = QUADRANT * quad + first
                nc.sync.dma_start(out=tile[top : top + SCALE_ROWS, :].bitcast(I32),
                                  in_=rows[SCALE_ROWS * quad : SCALE_ROWS * (quad + 1), :])
            return tile[first:P, :]

        def load_e4m3_words(name, words):
            tile = held.tile([P, POOL], U32, name=name, align_bytes=64)
            nc.sync.dma_start(out=tile[:].bitcast(I32),
                              in_=words[0].rearrange("p n t -> p (n t)").bitcast(I32))
            return tile

        def load_list(name, src):
            tile = held.tile([P, LIST_COLS], U16, name=name)
            nc.sync.dma_start(tile[:], src)
            return tile

        def list_half(tile, h):
            return tile[:, h * LIST_COLS // 2 : (h + 1) * LIST_COLS // 2]

        def slot_half(h):
            return slice(h * HALF, (h + 1) * HALF)

        q_raw = held.tile([P, PACK, P], F32, name="q_raw")
        nc.sync.dma_start(out=q_raw[:], in_=query.rearrange("(p t) q -> p t q", t=PACK))
        notes_sc = load_scales("notes_sc", notes_scales, 0)
        notes_w = held.tile([P, 2 * POOL], U8, name="notes_w", align_bytes=64)
        nc.sync.dma_start(out=notes_w[:].bitcast(I32), in_=notes_words[0].bitcast(I32))
        keys_w = load_e4m3_words("keys_w", keys_words)
        keys_sc = load_scales("keys_sc", keys_scales, SCALE_ROWS)
        idx2 = load_list("idx2", offs2)
        idx = load_list("idx", offs)
        idx3 = load_list("idx3", offs3)
        users_w = load_e4m3_words("users_w", users_words)
        users_sc = load_scales("users_sc", users_scales, 2 * SCALE_ROWS)
        idx5 = load_list("idx5", offs5)
        idx4 = load_list("idx4", offs4)
        idx6 = load_list("idx6", offs6)

        f1 = held.tile([P, POOL], F32, name="f1")
        f2 = held.tile([P, POOL], F32, name="f2")
        nc.vector.memset(f1[:], 0.0)
        nc.vector.memset(f2[:], 0.0)

        q_bf = held.tile([P, P, PACK], BF16, name="q_bf", align_bytes=64)
        q_w = held.tile([P, P], U32, name="q_w", align_bytes=64)
        q_sc = held.tile([P, P], U8, name="q_sc", align_bytes=64)
        row_halves = [slice(0, P // 2), slice(P // 2, P)]
        for rows in row_halves:
            nc.vector.tensor_copy(out=q_bf[:, rows, :], in_=q_raw[:, :, rows].rearrange("p t q -> p q t"))
        for rows in row_halves:
            nc.vector.quantize_mx(out=q_w[:, rows].bitcast(FP8X4), scales=q_sc[:, rows],
                                  in_=q_bf[:, rows, :].rearrange("p q t -> p (q t)"))

        def score(bank_name, words, scales):
            bank = psum.tile([P, scales.shape[1]], F32, name=bank_name)
            nc.tensor.matmul_mx(out=bank[:], lhsT=q_w[:].bitcast(FP8X4), lhsT_scale=q_sc[:],
                                rhs=words, rhs_scale=scales, start=True, stop=True)
            return bank

        pieces = [slice(0, BANK), slice(BANK, POOL - TAIL), slice(POOL - TAIL, POOL)]
        b_ps = [score("b%d" % n, notes_w[:, 2 * cols.start : 2 * cols.stop].bitcast(FP4X4), notes_sc[:, cols])
                for n, cols in enumerate(pieces)]
        quarters = [slice(lo, lo + POOL // 4) for lo in range(0, POOL, POOL // 4)]
        a_ps = [score("ac%d" % n, keys_w[:, cols].bitcast(FP8X4), keys_sc[:, cols])
                for n, cols in enumerate(quarters)]

        a = held.tile([P, POOL], F32, name="a")
        b = held.tile([P, POOL], F32, name="b")
        c0 = held.tile([P, POOL], F32, name="c0")
        a_got = [held.tile([P, HALF], F32, name="a_got%d" % h) for h in range(2)]
        b_got = held.tile([P, SLOTS], F32, name="b_got")
        m1 = held.tile([P, SLOTS], F32, name="m1")

        nc.scalar.copy(out=b[:, pieces[0]], in_=b_ps[0][:])
        nc.vector.tensor_copy(out=b[:, pieces[1]], in_=b_ps[1][:])
        nc.scalar.copy(out=b[:, pieces[2]], in_=b_ps[2][:])
        nc.scalar.activation(b_got[:], b[:].indirect(idx2[:]), COPY)
        for cols, bank in zip(quarters, a_ps):
            nc.vector.tensor_copy(out=a[:, cols], in_=bank[:])
        nc.scalar.activation(a_got[0][:], a[:].indirect(list_half(idx, 0)), COPY)
        nc.vector.tensor_copy(a_got[1][:], a[:].indirect(list_half(idx, 1)))
        for h in range(2):
            nc.vector.tensor_tensor(m1[:, slot_half(h)], a_got[h][:], b_got[:, slot_half(h)], MAX)
        nc.vector.tensor_copy(f1[:].indirect(idx3[:]), m1[:])

        banks = [slice(0, BANK), slice(BANK, POOL)]
        c_ps = [score("ac%d" % n, users_w[:, cols].bitcast(FP8X4), users_sc[:, cols])
                for n, cols in enumerate(banks)]

        c0_got = held.tile([P, SLOTS], F32, name="c0_got")
        c0_tail = held.tile([P, TAIL], F32, name="c0_tail")
        for cols, bank in zip(banks, c_ps):
            nc.scalar.copy(out=c0[:, cols], in_=bank[:])
        nc.scalar.activation(c0_got[:], c0[:].indirect(idx5[:]), COPY)
        nc.scalar.copy(out=c0_tail[:], in_=c_ps[1][:, BANK - TAIL : BANK])

        bb = held.tile([P, POOL], F32, name="bb")
        nc.gpsimd.tensor_tensor(bb[:, pieces[2]], b[:, pieces[2]], f1[:, pieces[2]], ADD)
        for n in range(2):
            nc.vector.tensor_tensor(bb[:, pieces[n]], b_ps[n][:], f1[:, pieces[n]], ADD)

        bb_got = [held.tile([P, HALF], F32, name=name) for name in ("c0", "bb_got1")]
        m2 = held.tile([P, SLOTS], F32, name="m2")
        nc.scalar.activation(bb_got[0][:], bb[:].indirect(list_half(idx4, 0)), COPY)
        nc.vector.tensor_copy(bb_got[1][:], bb[:].indirect(list_half(idx4, 1)))
        for h in range(2):
            nc.vector.tensor_tensor(m2[:, slot_half(h)], bb_got[h][:], c0_got[:, slot_half(h)], MAX)
        nc.vector.tensor_copy(f2[:].indirect(idx6[:]), m2[:])

        cc = held.tile([P, POOL], F32, name="cc")
        nc.gpsimd.tensor_tensor(cc[:, pieces[2]], c0_tail[:], f2[:, pieces[2]], ADD)
        nc.vector.tensor_tensor(cc[:, pieces[0]], c_ps[0][:], f2[:, pieces[0]], ADD)
        nc.vector.tensor_tensor(cc[:, pieces[1]], c_ps[1][:, 0 : BANK - TAIL], f2[:, pieces[1]], ADD)
        result = [held.tile([P, HALF], F32, name="result%d" % h) for h in range(2)]
        nc.vector.tensor_copy(result[0][:], cc[:].indirect(list_half(idx5, 0)))
        nc.scalar.activation(result[1][:], cc[:].indirect(list_half(idx5, 1)), COPY)
        nc.sync.dma_start(out=out[:, slot_half(0)], in_=result[0][:])
        nc.scalar.dma_start(out=out[:, slot_half(1)], in_=result[1][:])
